import numpy as np
import ml_dtypes


def mxq(x, axis, fmt="e4m3"):
    dtype, down = {"e4m3": (ml_dtypes.float8_e4m3fn, 7), "e5m2": (ml_dtypes.float8_e5m2, 14)}[fmt]
    v = np.moveaxis(np.asarray(x, np.float32).astype(ml_dtypes.bfloat16).astype(np.float64), axis, -1)
    blocks = v.reshape(v.shape[:-1] + (-1, 32))
    amax = np.abs(blocks).max(-1, keepdims=True)
    byte = np.maximum(np.where(amax > 0, np.frexp(amax)[1] - 1 + 127, 0) - down, 1)
    scale = np.exp2(byte - 127.0)
    codes = (blocks / scale).astype(np.float32).astype(dtype).astype(np.float64)
    return np.moveaxis((codes * scale).reshape(v.shape), -1, axis)


WIDE = False


def mx_kscale(k):
    if not WIDE:
        return np.ones(k)
    levels = np.array([10, -10, 5, -5, 0])
    if k % 512:
        return np.exp2(np.random.permutation(np.resize(levels, k // 32))).repeat(32)
    a = np.empty((k // 512, 16))
    for p in range(k // 512):
        a[p, :8] = np.random.permutation(np.resize(levels, 8))
        for g in range(8):
            far = levels[np.abs(levels - a[p, g]) >= 10]
            a[p, g + 8] = far[np.random.randint(len(far))]
    return np.exp2(a.ravel()).repeat(32)


def f64(x):
    return np.asarray(x).astype(np.float64)


def striped(idx):
    return np.tile(idx.reshape(-1, 16).T, (8, 1)).astype(np.uint16)


def unstriped(offs):
    return offs[:16].T.reshape(-1).astype(np.int64)


def pack_weight(w):
    k, n = w.shape
    w = f64(np.asarray(w, np.float32).astype(ml_dtypes.bfloat16)).reshape(k // 32, 32, n)
    amax = np.abs(w).max(1)
    byte = np.clip(np.where(amax > 0, np.frexp(amax)[1] - 1 + 127 - 7, 1), 1, 254)
    scaled = (w * np.exp2(127.0 - byte)[:, None, :]).reshape(k, n).astype(np.float32)
    words = np.ascontiguousarray(scaled.reshape(k // 512, 128, 4, n).transpose(0, 1, 3, 2)).astype(ml_dtypes.float8_e4m3fn).view(np.uint8)
    return words, np.ascontiguousarray(byte.astype(np.uint8).reshape(k // 512, 16, n))


def unpack_weight(words, scales):
    g, p, n, _ = words.shape
    vals = np.ascontiguousarray(words).view(ml_dtypes.float8_e4m3fn).astype(np.float64) * np.repeat(np.exp2(scales.astype(np.float64) - 127.0), 8, axis=1)[..., None]
    return vals.transpose(0, 1, 3, 2).reshape(g * 512, n)


def silu(v):
    return v / (1.0 + np.exp(-np.maximum(v, -700.0)))


K, T, S, D, H, N = 512, 4096, 1024, 2, 512, 256


def setup_inputs():
    n = np.random.standard_normal
    s = mx_kscale(K)[:, None]
    u = mx_kscale(H)
    packed_xT = pack_weight(n((K, T)) * s)
    packed_w2 = pack_weight(n((H, N)) / np.sqrt(H) / u[:, None])
    return {
        "x_words": packed_xT[0],
        "x_scales": packed_xT[1],
        "w1": (n((K, H)) / np.sqrt(K) / s * u).astype(np.float32),
        "w2_words": packed_w2[0],
        "w2_scales": packed_w2[1],
        "taps": (n((H, D)) / np.sqrt(D)).astype(np.float32),
        "offs": striped(np.random.permutation(T)[:S]),
    }


def reference(x_words, x_scales, w1, w2_words, w2_scales, taps, offs):
    xq = unpack_weight(x_words, x_scales)[:, unstriped(offs)]
    h = mxq(f64(w1), 0, "e4m3").T @ xq
    z = silu(f64(taps)[:, 0:1] * h + f64(taps)[:, 1:2] * (np.pad(h, ((0, 0), (1, 0)))[:, :S]))
    return unpack_weight(w2_words, w2_scales).T @ mxq(z, 0, "e4m3")

@@ -1,0 +1,220 @@
+from contextlib import ExitStack
+
+import concourse.mybir as mybir
+
+K, T, S, H, N = 512, 4096, 1024, 512, 256
+FLOPS = 2 * K * H * S + 2 * H * N * S
+
+F32 = mybir.dt.float32
+BF16 = mybir.dt.bfloat16
+I32 = mybir.dt.int32
+U32 = mybir.dt.uint32
+U16 = mybir.dt.uint16
+U8 = mybir.dt.uint8
+FP8X4 = mybir.dt.float8_e4m3fn_x4
+MULT = mybir.AluOpType.mult
+ADD = mybir.AluOpType.add
+COPY = mybir.ActivationFunctionType.Copy
+SILU = mybir.ActivationFunctionType.Silu
+
+P = 128
+PACK = 4
+HALF = 512
+PAD = 4
+X_HEAD = 1024
+W1_CHUNK = 256
+VECTOR_BANKS = (1, 5)
+PIECES = ((0, 256), (256, 256), (512, 256), (768, 128), (896, 128))
+
+
+def tile_picked_dconv_silu_p_kernel(
+    tc, x_words, x_scales, w1, w2_words, w2_scales, taps, offs, out
+):
+    nc = tc.nc
+    with ExitStack() as ctx:
+        keep = ctx.enter_context(tc.tile_pool(name="keep", bufs=1))
+        psum = ctx.enter_context(tc.psum_pool(name="psum", bufs=8))
+
+        offsets = keep.tile([P, S // 16], U16, name="offsets")
+        nc.sync.dma_start(offsets[:], offs)
+
+        word_table = keep.tile([P, T], U32, name="word_table", align_bytes=64)
+        x_rows = x_words[0].rearrange("p c r -> p (c r)").bitcast(I32)
+        nc.sync.dma_start(word_table[:].bitcast(I32)[:, 0:X_HEAD], x_rows[:, 0:X_HEAD])
+
+        scale_table = keep.tile([P, T], U8, name="scale_table", align_bytes=64)
+        nc.vector.memset(scale_table[:].bitcast(I32), 0)
+        nc.sync.dma_start(scale_table[:].bitcast(I32)[0:P:8, :], x_scales[0].bitcast(I32))
+
+        nc.sync.dma_start(word_table[:].bitcast(I32)[:, X_HEAD:T], x_rows[:, X_HEAD:T])
+
+        w1_rows = w1.rearrange("(p j) c -> p j c", j=PACK)
+        w1_raw = []
+        for c in range(2):
+            raw = keep.tile([P, PACK, W1_CHUNK], F32, name="w1_raw%d" % c, tag="w1_raw%d" % c, align_bytes=64)
+            nc.sync.dma_start(raw[:], w1_rows[:, :, c * W1_CHUNK : (c + 1) * W1_CHUNK])
+            w1_raw.append(raw)
+
+        tap_cols = keep.tile([P, PACK, 2], F32, name="tap_cols")
+        nc.gpsimd.dma_start(tap_cols[:], taps.rearrange("(p t) d -> p t d", t=PACK))
+
+        w2_plane = keep.tile([P, N], U8, name="w2_plane", align_bytes=64)
+        nc.vector.memset(w2_plane[:].bitcast(I32), 0)
+        for q in range(4):
+            nc.gpsimd.dma_start(
+                w2_plane[:].bitcast(I32)[32 * q : 32 * q + 4, :], w2_scales[0].bitcast(I32)[4 * q : 4 * q + 4, :]
+            )
+
+        x_plane = keep.tile([P, S], U8, name="x_plane", align_bytes=64)
+        nc.vector.memset(x_plane[:].bitcast(I32), 0)
+
+        lagged = keep.tile([P, PACK, PAD + S], F32, name="lagged", align_bytes=64)
+        zeros = keep.tile([P, PACK, PAD], F32, name="zeros")
+        nc.vector.memset(zeros[:], 0.0)
+        nc.scalar.activation(lagged[:, :, 0:PAD], zeros[:], SILU)
+
+        picked_scales = keep.tile([P, S], U8, name="picked_scales", align_bytes=64)
+        nc.vector.tensor_copy(picked_scales[:], scale_table[:].indirect(offsets[:]))
+        for q in range(4):
+            nc.scalar.dma_start(
+                x_plane[:].bitcast(I32)[32 * q : 32 * q + 4, :],
+                picked_scales[:].bitcast(I32)[32 * q : 32 * q + 32 : 8, :],
+            )
+
+        picked = []
+        for half in range(2):
+            words = keep.tile([P, HALF], U32, name="picked%d" % half, align_bytes=64)
+            cols = slice(half * HALF // 16, (half + 1) * HALF // 16)
+            nc.vector.tensor_copy(words[:], word_table[:].indirect(offsets[:, cols]))
+            picked.append(words)
+
+        w1_grouped = keep.tile([P, PACK, P, PACK], BF16, name="w1_grouped", align_bytes=64)
+        m_chunk = W1_CHUNK // PACK
+        for c in range(2):
+            dst = w1_grouped[:, :, c * m_chunk : (c + 1) * m_chunk, :].rearrange("p t m j -> p m j t")
+            src = w1_raw[c][:].rearrange("p j (m t) -> p m j t", t=PACK)
+            if c == 0:
+                nc.scalar.copy(dst, src)
+            else:
+                nc.vector.tensor_copy(dst, src)
+
+        w2_codes = keep.tile([P, N], U32, name="w2_codes", tag="w1_raw0", align_bytes=64)
+        nc.sync.dma_start(
+            w2_codes[:].bitcast(I32), w2_words[0].rearrange("p c r -> p (c r)").bitcast(I32)
+        )
+
+        w1_codes = keep.tile([P, PACK, P], U32, name="w1_codes", align_bytes=64)
+        w1_plane = keep.tile([P, PACK, P], U8, name="w1_plane", align_bytes=64)
+        for t in range(PACK):
+            nc.vector.quantize_mx(
+                out=w1_codes[:, t, :].bitcast(FP8X4),
+                scales=w1_plane[:, t, :],
+                in_=w1_grouped[:, t, :, :].rearrange("p m j -> p (m j)"),
+            )
+
+        banks = []
+        for b in range(8):
+            half, t = divmod(b, PACK)
+            h = psum.tile([P, HALF], F32, name="h%d" % b, tag="bank")
+            nc.tensor.matmul_mx(
+                out=h[:],
+                lhsT=w1_codes[:, t, :].bitcast(FP8X4),
+                lhsT_scale=w1_plane[:, t, :],
+                rhs=picked[half][:].bitcast(FP8X4),
+                rhs_scale=x_plane[:, half * HALF : (half + 1) * HALF],
+                start=True,
+                stop=True,
+            )
+            banks.append(h)
+
+        conv = [keep.tile([P, PACK, HALF], F32, name="conv%d" % half, align_bytes=64) for half in range(2)]
+
+        def lag(b):
+            half, t = divmod(b, PACK)
+            dst = lagged[:, t, PAD + half * HALF : PAD + (half + 1) * HALF]
+            if b in VECTOR_BANKS:
+                nc.vector.tensor_scalar(dst, banks[b][:], tap_cols[:, t, 1:2], None, MULT)
+            else:
+                nc.scalar.activation(dst, banks[b][:], COPY, scale=tap_cols[:, t, 1:2])
+
+        def combine(b):
+            half, t = divmod(b, PACK)
+            nc.vector.scalar_tensor_tensor(
+                conv[half][:, t, :],
+                banks[b][:],
+                tap_cols[:, t, 0:1],
+                lagged[:, t, PAD - 1 + half * HALF : PAD - 1 + (half + 1) * HALF],
+                MULT,
+                ADD,
+            )
+
+        for half in range(2):
+            for t in range(PACK):
+                lag(PACK * half + t)
+            for t in range(PACK):
+                combine(PACK * half + t)
+
+        z_tiles, products = {}, {}
+
+        def silu(i):
+            j0, n = PIECES[i]
+            z = keep.tile([P, n, PACK], BF16, name="z%d" % i, align_bytes=64)
+            nc.scalar.activation(
+                z[:].rearrange("p (c i) t -> p c t i", i=4),
+                conv[j0 // HALF][:, :, j0 % HALF : j0 % HALF + n].rearrange("p t (c i) -> p c t i", i=4),
+                SILU,
+            )
+            z_tiles[i] = z
+
+        def project(i):
+            j0, n = PIECES[i]
+            codes = keep.tile([P, n], U32, name="z_codes%d" % i, align_bytes=64)
+            plane = keep.tile([P, n], U8, name="z_plane%d" % i, align_bytes=64)
+            nc.vector.quantize_mx(
+                out=codes[:].bitcast(FP8X4), scales=plane[:], in_=z_tiles[i][:].rearrange("p n t -> p (n t)")
+            )
+            if i == len(PIECES) - 1:
+                accs = [psum.tile([P, HALF], F32, name="y%d_%d" % (i, m), tag="bank")[:, 0:n] for m in range(2)]
+            else:
+                y = psum.tile([P, HALF], F32, name="y%d" % i, tag="bank")
+                accs = [y[:, m * n : (m + 1) * n] for m in range(2)] + [y[:, 0 : 2 * n]]
+            for m in range(2):
+                nc.tensor.matmul_mx(
+                    out=accs[m],
+                    lhsT=w2_codes[:, m * P : (m + 1) * P].bitcast(FP8X4),
+                    lhsT_scale=w2_plane[:, m * P : (m + 1) * P],
+                    rhs=codes[:].bitcast(FP8X4),
+                    rhs_scale=plane[:],
+                    start=True,
+                    stop=True,
+                )
+            products[i] = accs
+
+        def store(i):
+            j0, n = PIECES[i]
+            staged = keep.tile([P, 2 * n], F32, name="staged%d" % i, align_bytes=64)
+            accs = products[i]
+            if i == len(PIECES) - 1:
+                nc.scalar.copy(staged[:, 0:n], accs[0])
+                nc.vector.tensor_copy(staged[:, n : 2 * n], accs[1])
+            elif i == len(PIECES) - 2:
+                nc.scalar.copy(staged[:], accs[2])
+            else:
+                nc.vector.tensor_copy(staged[:], accs[2])
+            nc.sync.dma_start(
+                out[:, j0 : j0 + n].rearrange("(m p) n -> p m n", p=P),
+                staged[:].rearrange("p (m n) -> p m n", m=2),
+            )
+
+        for i in range(len(PIECES)):
+            silu(i)
+        project(0)
+        project(1)
+        store(0)
+        project(2)
+        store(1)
+        project(3)
+        project(4)
+        store(2)
+        store(3)
+        store(4)

@@ -21,10 +21,11 @@ P = 128
 PACK = 4
 HALF = 512
 PAD = 4
-X_HEAD = 1024
-W1_CHUNK = 256
-VECTOR_BANKS = (1, 5)
-PIECES = ((0, 256), (256, 256), (512, 256), (768, 128), (896, 128))
+WARM_PASSES = 3
+VECTOR_BANKS = (1, 7)
+SPANS = ((0, 512), (512, 256), (768, 256))
+PIECES = ((0, 256), (256, 256), (512, 128), (640, 128), (768, 128), (896, 128))
+WAY_OUT = ("vector", "both", "scalar", "vector", "scalar", "both")
 
 
 def tile_picked_dconv_silu_p_kernel(
@@ -38,22 +39,20 @@ def tile_picked_dconv_silu_p_kernel(
         offsets = keep.tile([P, S // 16], U16, name="offsets")
         nc.sync.dma_start(offsets[:], offs)
 
-        word_table = keep.tile([P, T], U32, name="word_table", align_bytes=64)
-        x_rows = x_words[0].rearrange("p c r -> p (c r)").bitcast(I32)
-        nc.sync.dma_start(word_table[:].bitcast(I32)[:, 0:X_HEAD], x_rows[:, 0:X_HEAD])
+        w1_rows = w1.rearrange("(p j) c -> p j c", j=PACK)
+        w1_raw = keep.tile([P, PACK, H], F32, name="w1_raw", tag="w1_raw", align_bytes=64)
+        nc.sync.dma_start(w1_raw[:, 0:2, :], w1_rows[:, 0:2, :])
 
         scale_table = keep.tile([P, T], U8, name="scale_table", align_bytes=64)
         nc.vector.memset(scale_table[:].bitcast(I32), 0)
         nc.sync.dma_start(scale_table[:].bitcast(I32)[0:P:8, :], x_scales[0].bitcast(I32))
 
-        nc.sync.dma_start(word_table[:].bitcast(I32)[:, X_HEAD:T], x_rows[:, X_HEAD:T])
+        nc.sync.dma_start(w1_raw[:, 2:4, :], w1_rows[:, 2:4, :])
 
-        w1_rows = w1.rearrange("(p j) c -> p j c", j=PACK)
-        w1_raw = []
-        for c in range(2):
-            raw = keep.tile([P, PACK, W1_CHUNK], F32, name="w1_raw%d" % c, tag="w1_raw%d" % c, align_bytes=64)
-            nc.sync.dma_start(raw[:], w1_rows[:, :, c * W1_CHUNK : (c + 1) * W1_CHUNK])
-            w1_raw.append(raw)
+        word_table = keep.tile([P, T], U32, name="word_table", align_bytes=64)
+        nc.sync.dma_start(
+            word_table[:].bitcast(I32), x_words[0].rearrange("p c r -> p (c r)").bitcast(I32)
+        )
 
         tap_cols = keep.tile([P, PACK, 2], F32, name="tap_cols")
         nc.gpsimd.dma_start(tap_cols[:], taps.rearrange("(p t) d -> p t d", t=PACK))
@@ -76,9 +75,39 @@ def tile_picked_dconv_silu_p_kernel(
         picked_scales = keep.tile([P, S], U8, name="picked_scales", align_bytes=64)
         nc.vector.tensor_copy(picked_scales[:], scale_table[:].indirect(offsets[:]))
         for q in range(4):
-            nc.scalar.dma_start(
+            nc.sync.dma_start(
                 x_plane[:].bitcast(I32)[32 * q : 32 * q + 4, :],
                 picked_scales[:].bitcast(I32)[32 * q : 32 * q + 32 : 8, :],
+            )
+
+        w1_grouped = keep.tile([P, PACK, P, PACK], BF16, name="w1_grouped", align_bytes=64)
+        w1_dst = w1_grouped[:].rearrange("p t m j -> p m j t")
+        w1_src = w1_raw[:].rearrange("p j (m t) -> p m j t", t=PACK)
+        nc.scalar.copy(w1_dst, w1_src)
+
+        w2_codes = keep.tile([P, N], U32, name="w2_codes", tag="w1_raw", align_bytes=64)
+        nc.sync.dma_start(
+            w2_codes[:].bitcast(I32), w2_words[0].rearrange("p c r -> p (c r)").bitcast(I32)
+        )
+
+        w1_codes = keep.tile([P, PACK, P], U32, name="w1_codes", align_bytes=64)
+        w1_plane = keep.tile([P, PACK, P], U8, name="w1_plane", align_bytes=64)
+        all_codes = w1_codes[:].rearrange("p t m -> p (t m)").bitcast(FP8X4)
+        all_scales = w1_plane[:].rearrange("p t m -> p (t m)")
+        nc.vector.quantize_mx(
+            out=all_codes, scales=all_scales, in_=w1_grouped[:].rearrange("p t m j -> p (t m j)")
+        )
+
+        banks = [psum.tile([P, HALF], F32, name="h%d" % b, tag="bank") for b in range(8)]
+        for b in range(8 - WARM_PASSES, 8):
+            nc.tensor.matmul_mx(
+                out=banks[b][:],
+                lhsT=w1_codes[:, 0, :].bitcast(FP8X4),
+                lhsT_scale=w1_plane[:, 0, :],
+                rhs=all_codes,
+                rhs_scale=all_scales,
+                start=True,
+                stop=True,
             )
 
         picked = []
@@ -88,36 +117,10 @@ def tile_picked_dconv_silu_p_kernel(
             nc.vector.tensor_copy(words[:], word_table[:].indirect(offsets[:, cols]))
             picked.append(words)
 
-        w1_grouped = keep.tile([P, PACK, P, PACK], BF16, name="w1_grouped", align_bytes=64)
-        m_chunk = W1_CHUNK // PACK
-        for c in range(2):
-            dst = w1_grouped[:, :, c * m_chunk : (c + 1) * m_chunk, :].rearrange("p t m j -> p m j t")
-            src = w1_raw[c][:].rearrange("p j (m t) -> p m j t", t=PACK)
-            if c == 0:
-                nc.scalar.copy(dst, src)
-            else:
-                nc.vector.tensor_copy(dst, src)
-
-        w2_codes = keep.tile([P, N], U32, name="w2_codes", tag="w1_raw0", align_bytes=64)
-        nc.sync.dma_start(
-            w2_codes[:].bitcast(I32), w2_words[0].rearrange("p c r -> p (c r)").bitcast(I32)
-        )
-
-        w1_codes = keep.tile([P, PACK, P], U32, name="w1_codes", align_bytes=64)
-        w1_plane = keep.tile([P, PACK, P], U8, name="w1_plane", align_bytes=64)
-        for t in range(PACK):
-            nc.vector.quantize_mx(
-                out=w1_codes[:, t, :].bitcast(FP8X4),
-                scales=w1_plane[:, t, :],
-                in_=w1_grouped[:, t, :, :].rearrange("p m j -> p (m j)"),
-            )
-
-        banks = []
         for b in range(8):
             half, t = divmod(b, PACK)
-            h = psum.tile([P, HALF], F32, name="h%d" % b, tag="bank")
             nc.tensor.matmul_mx(
-                out=h[:],
+                out=banks[b][:],
                 lhsT=w1_codes[:, t, :].bitcast(FP8X4),
                 lhsT_scale=w1_plane[:, t, :],
                 rhs=picked[half][:].bitcast(FP8X4),
@@ -125,9 +128,8 @@ def tile_picked_dconv_silu_p_kernel(
                 start=True,
                 stop=True,
             )
-            banks.append(h)
 
-        conv = [keep.tile([P, PACK, HALF], F32, name="conv%d" % half, align_bytes=64) for half in range(2)]
+        conv = [keep.tile([P, PACK, n], F32, name="conv%d" % j0, align_bytes=64) for j0, n in SPANS]
 
         def lag(b):
             half, t = divmod(b, PACK)
@@ -137,31 +139,35 @@ def tile_picked_dconv_silu_p_kernel(
             else:
                 nc.scalar.activation(dst, banks[b][:], COPY, scale=tap_cols[:, t, 1:2])
 
-        def combine(b):
-            half, t = divmod(b, PACK)
-            nc.vector.scalar_tensor_tensor(
-                conv[half][:, t, :],
-                banks[b][:],
-                tap_cols[:, t, 0:1],
-                lagged[:, t, PAD - 1 + half * HALF : PAD - 1 + (half + 1) * HALF],
-                MULT,
-                ADD,
-            )
+        def combine(s):
+            j0, n = SPANS[s]
+            for t in range(PACK):
+                nc.vector.scalar_tensor_tensor(
+                    conv[s][:, t, :],
+                    banks[PACK * (j0 // HALF) + t][:, j0 % HALF : j0 % HALF + n],
+                    tap_cols[:, t, 0:1],
+                    lagged[:, t, PAD - 1 + j0 : PAD - 1 + j0 + n],
+                    MULT,
+                    ADD,
+                )
 
-        for half in range(2):
-            for t in range(PACK):
-                lag(PACK * half + t)
-            for t in range(PACK):
-                combine(PACK * half + t)
+        for b in range(PACK):
+            lag(b)
+        combine(0)
+        for b in range(PACK, 2 * PACK):
+            lag(b)
+        combine(1)
 
         z_tiles, products = {}, {}
 
         def silu(i):
             j0, n = PIECES[i]
+            s = max(s for s in range(len(SPANS)) if SPANS[s][0] <= j0)
+            c0 = j0 - SPANS[s][0]
             z = keep.tile([P, n, PACK], BF16, name="z%d" % i, align_bytes=64)
             nc.scalar.activation(
                 z[:].rearrange("p (c i) t -> p c t i", i=4),
-                conv[j0 // HALF][:, :, j0 % HALF : j0 % HALF + n].rearrange("p t (c i) -> p c t i", i=4),
+                conv[s][:, :, c0 : c0 + n].rearrange("p t (c i) -> p c t i", i=4),
                 SILU,
             )
             z_tiles[i] = z
@@ -173,7 +179,7 @@ def tile_picked_dconv_silu_p_kernel(
             nc.vector.quantize_mx(
                 out=codes[:].bitcast(FP8X4), scales=plane[:], in_=z_tiles[i][:].rearrange("p n t -> p (n t)")
             )
-            if i == len(PIECES) - 1:
+            if WAY_OUT[i] == "both":
                 accs = [psum.tile([P, HALF], F32, name="y%d_%d" % (i, m), tag="bank")[:, 0:n] for m in range(2)]
             else:
                 y = psum.tile([P, HALF], F32, name="y%d" % i, tag="bank")
@@ -194,10 +200,10 @@ def tile_picked_dconv_silu_p_kernel(
             j0, n = PIECES[i]
             staged = keep.tile([P, 2 * n], F32, name="staged%d" % i, align_bytes=64)
             accs = products[i]
-            if i == len(PIECES) - 1:
+            if WAY_OUT[i] == "both":
                 nc.scalar.copy(staged[:, 0:n], accs[0])
                 nc.vector.tensor_copy(staged[:, n : 2 * n], accs[1])
-            elif i == len(PIECES) - 2:
+            elif WAY_OUT[i] == "scalar":
                 nc.scalar.copy(staged[:], accs[2])
             else:
                 nc.vector.tensor_copy(staged[:], accs[2])
@@ -206,15 +212,20 @@ def tile_picked_dconv_silu_p_kernel(
                 staged[:].rearrange("p (m n) -> p m n", m=2),
             )
 
-        for i in range(len(PIECES)):
-            silu(i)
+        silu(0)
         project(0)
+        combine(2)
+        silu(1)
         project(1)
+        silu(2)
         store(0)
         project(2)
-        store(1)
+        silu(3)
         project(3)
+        store(1)
+        silu(4)
         project(4)
-        store(2)
-        store(3)
-        store(4)
+        silu(5)
+        project(5)
+        for i in range(2, 6):
+            store(i)

@@ -25,7 +25,7 @@ WARM_PASSES = 3
 VECTOR_BANKS = (1, 7)
 SPANS = ((0, 512), (512, 256), (768, 256))
 PIECES = ((0, 256), (256, 256), (512, 128), (640, 128), (768, 128), (896, 128))
-WAY_OUT = ("vector", "both", "scalar", "vector", "scalar", "both")
+WAY_OUT = ("vector", "vector", "scalar", "scalar", "both", "both")
 
 
 def tile_picked_dconv_silu_p_kernel(
@@ -36,14 +36,14 @@ def tile_picked_dconv_silu_p_kernel(
         keep = ctx.enter_context(tc.tile_pool(name="keep", bufs=1))
         psum = ctx.enter_context(tc.psum_pool(name="psum", bufs=8))
 
-        offsets = keep.tile([P, S // 16], U16, name="offsets")
-        nc.sync.dma_start(offsets[:], offs)
-
         w1_rows = w1.rearrange("(p j) c -> p j c", j=PACK)
         w1_raw = keep.tile([P, PACK, H], F32, name="w1_raw", tag="w1_raw", align_bytes=64)
         nc.sync.dma_start(w1_raw[:, 0:2, :], w1_rows[:, 0:2, :])
 
-        scale_table = keep.tile([P, T], U8, name="scale_table", align_bytes=64)
+        offsets = keep.tile([P, S // 16], U16, name="offsets")
+        nc.sync.dma_start(offsets[:], offs)
+
+        scale_table = keep.tile([P, T], U8, name="scale_table", tag="scale_table", align_bytes=64)
         nc.vector.memset(scale_table[:].bitcast(I32), 0)
         nc.sync.dma_start(scale_table[:].bitcast(I32)[0:P:8, :], x_scales[0].bitcast(I32))
 
@@ -55,14 +55,7 @@ def tile_picked_dconv_silu_p_kernel(
         )
 
         tap_cols = keep.tile([P, PACK, 2], F32, name="tap_cols")
-        nc.gpsimd.dma_start(tap_cols[:], taps.rearrange("(p t) d -> p t d", t=PACK))
-
-        w2_plane = keep.tile([P, N], U8, name="w2_plane", align_bytes=64)
-        nc.vector.memset(w2_plane[:].bitcast(I32), 0)
-        for q in range(4):
-            nc.gpsimd.dma_start(
-                w2_plane[:].bitcast(I32)[32 * q : 32 * q + 4, :], w2_scales[0].bitcast(I32)[4 * q : 4 * q + 4, :]
-            )
+        nc.scalar.dma_start(tap_cols[:], taps.rearrange("(p t) d -> p t d", t=PACK))
 
         x_plane = keep.tile([P, S], U8, name="x_plane", align_bytes=64)
         nc.vector.memset(x_plane[:].bitcast(I32), 0)
@@ -80,10 +73,18 @@ def tile_picked_dconv_silu_p_kernel(
                 picked_scales[:].bitcast(I32)[32 * q : 32 * q + 32 : 8, :],
             )
 
+        w2_plane = keep.tile([P, N], U8, name="w2_plane", tag="scale_table", align_bytes=64)
+        nc.vector.memset(w2_plane[:].bitcast(I32), 0)
+        for q in range(4):
+            nc.sync.dma_start(
+                w2_plane[:].bitcast(I32)[32 * q : 32 * q + 4, :], w2_scales[0].bitcast(I32)[4 * q : 4 * q + 4, :]
+            )
+
         w1_grouped = keep.tile([P, PACK, P, PACK], BF16, name="w1_grouped", align_bytes=64)
         w1_dst = w1_grouped[:].rearrange("p t m j -> p m j t")
         w1_src = w1_raw[:].rearrange("p j (m t) -> p m j t", t=PACK)
-        nc.scalar.copy(w1_dst, w1_src)
+        nc.scalar.copy(w1_dst[:, :, :, 0:3], w1_src[:, :, :, 0:3])
+        nc.vector.tensor_copy(w1_grouped[:, 3, :, :], w1_src[:, :, :, 3])
 
         w2_codes = keep.tile([P, N], U32, name="w2_codes", tag="w1_raw", align_bytes=64)
         nc.sync.dma_start(
@@ -214,16 +215,16 @@ def tile_picked_dconv_silu_p_kernel(
 
         silu(0)
         project(0)
-        combine(2)
         silu(1)
         project(1)
+        combine(2)
         silu(2)
         store(0)
         project(2)
         silu(3)
         project(3)
-        store(1)
         silu(4)
+        store(1)
         project(4)
         silu(5)
         project(5)

@@ -24,8 +24,8 @@ PAD = 4
 WARM_PASSES = 3
 VECTOR_BANKS = (1, 7)
 SPANS = ((0, 512), (512, 256), (768, 256))
-PIECES = ((0, 256), (256, 256), (512, 128), (640, 128), (768, 128), (896, 128))
-WAY_OUT = ("vector", "vector", "scalar", "scalar", "both", "both")
+PIECES = tuple((128 * i, 128) for i in range(8))
+WAY_OUT = ("vector",) * 4 + ("scalar",) * 3 + ("both",)
 
 
 def tile_picked_dconv_silu_p_kernel(
@@ -213,20 +213,10 @@ def tile_picked_dconv_silu_p_kernel(
                 staged[:].rearrange("p (m n) -> p m n", m=2),
             )
 
-        silu(0)
-        project(0)
-        silu(1)
-        project(1)
-        combine(2)
-        silu(2)
-        store(0)
-        project(2)
-        silu(3)
-        project(3)
-        silu(4)
-        store(1)
-        project(4)
-        silu(5)
-        project(5)
-        for i in range(2, 6):
+        for i in range(len(PIECES)):
+            if i == 2:
+                combine(2)
+            silu(i)
+            project(i)
+        for i in range(len(PIECES)):
             store(i)

@@ -22,6 +22,7 @@ PACK = 4
 HALF = 512
 PAD = 4
 WARM_PASSES = 3
+ROW0, ROW_STEP = 11, 7
 VECTOR_BANKS = (1, 7)
 SPANS = ((0, 512), (512, 256), (768, 256))
 PIECES = tuple((128 * i, 128) for i in range(8))
@@ -45,7 +46,7 @@ def tile_picked_dconv_silu_p_kernel(
 
         scale_table = keep.tile([P, T], U8, name="scale_table", tag="scale_table", align_bytes=64)
         nc.vector.memset(scale_table[:].bitcast(I32), 0)
-        nc.sync.dma_start(scale_table[:].bitcast(I32)[0:P:8, :], x_scales[0].bitcast(I32))
+        nc.sync.dma_start(scale_table[:].bitcast(I32)[ROW0 : ROW0 + 16 * ROW_STEP : ROW_STEP, :], x_scales[0].bitcast(I32))
 
         nc.sync.dma_start(w1_raw[:, 2:4, :], w1_rows[:, 2:4, :])
 
@@ -70,7 +71,7 @@ def tile_picked_dconv_silu_p_kernel(
         for q in range(4):
             nc.sync.dma_start(
                 x_plane[:].bitcast(I32)[32 * q : 32 * q + 4, :],
-                picked_scales[:].bitcast(I32)[32 * q : 32 * q + 32 : 8, :],
+                picked_scales[:].bitcast(I32)[ROW0 + 4 * q * ROW_STEP : ROW0 + 4 * (q + 1) * ROW_STEP : ROW_STEP, :],
             )
 
         w2_plane = keep.tile([P, N], U8, name="w2_plane", tag="scale_table", align_bytes=64)

@@ -21,7 +21,8 @@ P = 128
 PACK = 4
 HALF = 512
 PAD = 4
-WARM_PASSES = 3
+WARM_PASSES = 22
+WARM_ROWS = 32
 ROW0, ROW_STEP = 11, 7
 VECTOR_BANKS = (1, 7)
 SPANS = ((0, 512), (512, 256), (768, 256))
@@ -81,11 +82,11 @@ def tile_picked_dconv_silu_p_kernel(
                 w2_plane[:].bitcast(I32)[32 * q : 32 * q + 4, :], w2_scales[0].bitcast(I32)[4 * q : 4 * q + 4, :]
             )
 
-        w1_grouped = keep.tile([P, PACK, P, PACK], BF16, name="w1_grouped", align_bytes=64)
-        w1_dst = w1_grouped[:].rearrange("p t m j -> p m j t")
         w1_src = w1_raw[:].rearrange("p j (m t) -> p m j t", t=PACK)
-        nc.scalar.copy(w1_dst[:, :, :, 0:3], w1_src[:, :, :, 0:3])
-        nc.vector.tensor_copy(w1_grouped[:, 3, :, :], w1_src[:, :, :, 3])
+        first_groups = keep.tile([P, PACK - 1, P, PACK], BF16, name="first_groups", align_bytes=64)
+        last_group = keep.tile([P, P, PACK], BF16, name="last_group", align_bytes=64)
+        nc.scalar.copy(first_groups[:].rearrange("p t m j -> p m j t"), w1_src[:, :, :, 0 : PACK - 1])
+        nc.vector.tensor_copy(last_group[:], w1_src[:, :, :, PACK - 1])
 
         w2_codes = keep.tile([P, N], U32, name="w2_codes", tag="w1_raw", align_bytes=64)
         nc.sync.dma_start(
@@ -94,20 +95,26 @@ def tile_picked_dconv_silu_p_kernel(
 
         w1_codes = keep.tile([P, PACK, P], U32, name="w1_codes", align_bytes=64)
         w1_plane = keep.tile([P, PACK, P], U8, name="w1_plane", align_bytes=64)
-        all_codes = w1_codes[:].rearrange("p t m -> p (t m)").bitcast(FP8X4)
-        all_scales = w1_plane[:].rearrange("p t m -> p (t m)")
         nc.vector.quantize_mx(
-            out=all_codes, scales=all_scales, in_=w1_grouped[:].rearrange("p t m j -> p (t m j)")
+            out=w1_codes[:, PACK - 1, :].bitcast(FP8X4),
+            scales=w1_plane[:, PACK - 1, :],
+            in_=last_group[:].rearrange("p m j -> p (m j)"),
         )
+        for t0, t1 in ((0, 2), (2, 3)):
+            nc.vector.quantize_mx(
+                out=w1_codes[:, t0:t1, :].rearrange("p t m -> p (t m)").bitcast(FP8X4),
+                scales=w1_plane[:, t0:t1, :].rearrange("p t m -> p (t m)"),
+                in_=first_groups[:, t0:t1, :, :].rearrange("p t m j -> p (t m j)"),
+            )
 
         banks = [psum.tile([P, HALF], F32, name="h%d" % b, tag="bank") for b in range(8)]
-        for b in range(8 - WARM_PASSES, 8):
+        for warm in range(WARM_PASSES):
             nc.tensor.matmul_mx(
-                out=banks[b][:],
-                lhsT=w1_codes[:, 0, :].bitcast(FP8X4),
-                lhsT_scale=w1_plane[:, 0, :],
-                rhs=all_codes,
-                rhs_scale=all_scales,
+                out=banks[7][0:WARM_ROWS, 0:P],
+                lhsT=w1_codes[:, PACK - 1, 0:WARM_ROWS].bitcast(FP8X4),
+                lhsT_scale=w1_plane[:, PACK - 1, 0:WARM_ROWS],
+                rhs=w1_codes[:, PACK - 1, :].bitcast(FP8X4),
+                rhs_scale=w1_plane[:, PACK - 1, :],
                 start=True,
                 stop=True,
             )

@@ -23,6 +23,8 @@ HALF = 512
 PAD = 4
 WARM_PASSES = 22
 WARM_ROWS = 32
+REWARM_AFTER = 1
+REWARM_PASSES = 6
 ROW0, ROW_STEP = 11, 7
 VECTOR_BANKS = (1, 7)
 SPANS = ((0, 512), (512, 256), (768, 256))
@@ -167,7 +169,7 @@ def tile_picked_dconv_silu_p_kernel(
             lag(b)
         combine(1)
 
-        z_tiles, products = {}, {}
+        z_tiles, products, early = {}, {}, {}
 
         def silu(i):
             j0, n = PIECES[i]
@@ -191,7 +193,9 @@ def tile_picked_dconv_silu_p_kernel(
             if WAY_OUT[i] == "both":
                 accs = [psum.tile([P, HALF], F32, name="y%d_%d" % (i, m), tag="bank")[:, 0:n] for m in range(2)]
             else:
-                y = psum.tile([P, HALF], F32, name="y%d" % i, tag="bank")
+                y = early.get(i)
+                if y is None:
+                    y = psum.tile([P, HALF], F32, name="y%d" % i, tag="bank")
                 accs = [y[:, m * n : (m + 1) * n] for m in range(2)] + [y[:, 0 : 2 * n]]
             for m in range(2):
                 nc.tensor.matmul_mx(
@@ -204,6 +208,19 @@ def tile_picked_dconv_silu_p_kernel(
                     stop=True,
                 )
             products[i] = accs
+            if i == REWARM_AFTER:
+                spare = psum.tile([P, HALF], F32, name="y%d" % (i + 1), tag="bank")
+                early[i + 1] = spare
+                for warm in range(REWARM_PASSES):
+                    nc.tensor.matmul_mx(
+                        out=spare[0:WARM_ROWS, 2 * n : 3 * n],
+                        lhsT=w2_codes[:, 0:WARM_ROWS].bitcast(FP8X4),
+                        lhsT_scale=w2_plane[:, 0:WARM_ROWS],
+                        rhs=codes[:].bitcast(FP8X4),
+                        rhs_scale=plane[:],
+                        start=True,
+                        stop=True,
+                    )
 
         def store(i):
             j0, n = PIECES[i]
@@ -211,7 +228,10 @@ def tile_picked_dconv_silu_p_kernel(
             accs = products[i]
             if WAY_OUT[i] == "both":
                 nc.scalar.copy(staged[:, 0:n], accs[0])
+                nc.sync.dma_start(out[0:P, j0 : j0 + n], staged[:, 0:n])
                 nc.vector.tensor_copy(staged[:, n : 2 * n], accs[1])
+                nc.sync.dma_start(out[P : 2 * P, j0 : j0 + n], staged[:, n : 2 * n])
+                return
             elif WAY_OUT[i] == "scalar":
                 nc.scalar.copy(staged[:], accs[2])
             else:

@@ -21,10 +21,8 @@ P = 128
 PACK = 4
 HALF = 512
 PAD = 4
-WARM_PASSES = 22
+WARM_PASSES = 3
 WARM_ROWS = 32
-REWARM_AFTER = 1
-REWARM_PASSES = 6
 ROW0, ROW_STEP = 11, 7
 VECTOR_BANKS = (1, 7)
 SPANS = ((0, 512), (512, 256), (768, 256))
@@ -41,19 +39,19 @@ def tile_picked_dconv_silu_p_kernel(
         psum = ctx.enter_context(tc.psum_pool(name="psum", bufs=8))
 
         w1_rows = w1.rearrange("(p j) c -> p j c", j=PACK)
-        w1_raw = keep.tile([P, PACK, H], F32, name="w1_raw", tag="w1_raw", align_bytes=64)
+        w1_raw = keep.tile([P, PACK, H], F32, name="w1_raw", tag="w1_raw", align_bytes=256)
         nc.sync.dma_start(w1_raw[:, 0:2, :], w1_rows[:, 0:2, :])
 
         offsets = keep.tile([P, S // 16], U16, name="offsets")
         nc.sync.dma_start(offsets[:], offs)
 
-        scale_table = keep.tile([P, T], U8, name="scale_table", tag="scale_table", align_bytes=64)
+        scale_table = keep.tile([P, T], U8, name="scale_table", tag="scale_table", align_bytes=256)
         nc.vector.memset(scale_table[:].bitcast(I32), 0)
         nc.sync.dma_start(scale_table[:].bitcast(I32)[ROW0 : ROW0 + 16 * ROW_STEP : ROW_STEP, :], x_scales[0].bitcast(I32))
 
         nc.sync.dma_start(w1_raw[:, 2:4, :], w1_rows[:, 2:4, :])
 
-        word_table = keep.tile([P, T], U32, name="word_table", align_bytes=64)
+        word_table = keep.tile([P, T], U32, name="word_table", align_bytes=256)
         nc.sync.dma_start(
             word_table[:].bitcast(I32), x_words[0].rearrange("p c r -> p (c r)").bitcast(I32)
         )
@@ -61,15 +59,15 @@ def tile_picked_dconv_silu_p_kernel(
         tap_cols = keep.tile([P, PACK, 2], F32, name="tap_cols")
         nc.scalar.dma_start(tap_cols[:], taps.rearrange("(p t) d -> p t d", t=PACK))
 
-        x_plane = keep.tile([P, S], U8, name="x_plane", align_bytes=64)
+        x_plane = keep.tile([P, S], U8, name="x_plane", align_bytes=256)
         nc.vector.memset(x_plane[:].bitcast(I32), 0)
 
-        lagged = keep.tile([P, PACK, PAD + S], F32, name="lagged", align_bytes=64)
+        lagged = keep.tile([P, PACK, PAD + S], F32, name="lagged", align_bytes=256)
         zeros = keep.tile([P, PACK, PAD], F32, name="zeros")
         nc.vector.memset(zeros[:], 0.0)
         nc.scalar.activation(lagged[:, :, 0:PAD], zeros[:], SILU)
 
-        picked_scales = keep.tile([P, S], U8, name="picked_scales", align_bytes=64)
+        picked_scales = keep.tile([P, S], U8, name="picked_scales", align_bytes=256)
         nc.vector.tensor_copy(picked_scales[:], scale_table[:].indirect(offsets[:]))
         for q in range(4):
             nc.sync.dma_start(
@@ -77,7 +75,7 @@ def tile_picked_dconv_silu_p_kernel(
                 picked_scales[:].bitcast(I32)[ROW0 + 4 * q * ROW_STEP : ROW0 + 4 * (q + 1) * ROW_STEP : ROW_STEP, :],
             )
 
-        w2_plane = keep.tile([P, N], U8, name="w2_plane", tag="scale_table", align_bytes=64)
+        w2_plane = keep.tile([P, N], U8, name="w2_plane", tag="scale_table", align_bytes=256)
         nc.vector.memset(w2_plane[:].bitcast(I32), 0)
         for q in range(4):
             nc.sync.dma_start(
@@ -85,18 +83,18 @@ def tile_picked_dconv_silu_p_kernel(
             )
 
         w1_src = w1_raw[:].rearrange("p j (m t) -> p m j t", t=PACK)
-        first_groups = keep.tile([P, PACK - 1, P, PACK], BF16, name="first_groups", align_bytes=64)
-        last_group = keep.tile([P, P, PACK], BF16, name="last_group", align_bytes=64)
+        first_groups = keep.tile([P, PACK - 1, P, PACK], BF16, name="first_groups", align_bytes=256)
+        last_group = keep.tile([P, P, PACK], BF16, name="last_group", align_bytes=256)
         nc.scalar.copy(first_groups[:].rearrange("p t m j -> p m j t"), w1_src[:, :, :, 0 : PACK - 1])
         nc.vector.tensor_copy(last_group[:], w1_src[:, :, :, PACK - 1])
 
-        w2_codes = keep.tile([P, N], U32, name="w2_codes", tag="w1_raw", align_bytes=64)
+        w2_codes = keep.tile([P, N], U32, name="w2_codes", tag="w1_raw", align_bytes=256)
         nc.sync.dma_start(
             w2_codes[:].bitcast(I32), w2_words[0].rearrange("p c r -> p (c r)").bitcast(I32)
         )
 
-        w1_codes = keep.tile([P, PACK, P], U32, name="w1_codes", align_bytes=64)
-        w1_plane = keep.tile([P, PACK, P], U8, name="w1_plane", align_bytes=64)
+        w1_codes = keep.tile([P, PACK, P], U32, name="w1_codes", align_bytes=256)
+        w1_plane = keep.tile([P, PACK, P], U8, name="w1_plane", align_bytes=256)
         nc.vector.quantize_mx(
             out=w1_codes[:, PACK - 1, :].bitcast(FP8X4),
             scales=w1_plane[:, PACK - 1, :],
@@ -112,18 +110,18 @@ def tile_picked_dconv_silu_p_kernel(
         banks = [psum.tile([P, HALF], F32, name="h%d" % b, tag="bank") for b in range(8)]
         for warm in range(WARM_PASSES):
             nc.tensor.matmul_mx(
-                out=banks[7][0:WARM_ROWS, 0:P],
-                lhsT=w1_codes[:, PACK - 1, 0:WARM_ROWS].bitcast(FP8X4),
-                lhsT_scale=w1_plane[:, PACK - 1, 0:WARM_ROWS],
-                rhs=w1_codes[:, PACK - 1, :].bitcast(FP8X4),
-                rhs_scale=w1_plane[:, PACK - 1, :],
+                out=banks[7][0:WARM_ROWS, :],
+                lhsT=w1_codes[:, 0, 0:WARM_ROWS].bitcast(FP8X4),
+                lhsT_scale=w1_plane[:, 0, 0:WARM_ROWS],
+                rhs=w1_codes[:].rearrange("p t m -> p (t m)").bitcast(FP8X4),
+                rhs_scale=w1_plane[:].rearrange("p t m -> p (t m)"),
                 start=True,
                 stop=True,
             )
 
         picked = []
         for half in range(2):
-            words = keep.tile([P, HALF], U32, name="picked%d" % half, align_bytes=64)
+            words = keep.tile([P, HALF], U32, name="picked%d" % half, align_bytes=256)
             cols = slice(half * HALF // 16, (half + 1) * HALF // 16)
             nc.vector.tensor_copy(words[:], word_table[:].indirect(offsets[:, cols]))
             picked.append(words)
@@ -140,7 +138,7 @@ def tile_picked_dconv_silu_p_kernel(
                 stop=True,
             )
 
-        conv = [keep.tile([P, PACK, n], F32, name="conv%d" % j0, align_bytes=64) for j0, n in SPANS]
+        conv = [keep.tile([P, PACK, n], F32, name="conv%d" % j0, align_bytes=256) for j0, n in SPANS]
 
         def lag(b):
             half, t = divmod(b, PACK)
@@ -169,13 +167,13 @@ def tile_picked_dconv_silu_p_kernel(
             lag(b)
         combine(1)
 
-        z_tiles, products, early = {}, {}, {}
+        z_tiles, products = {}, {}
 
         def silu(i):
             j0, n = PIECES[i]
             s = max(s for s in range(len(SPANS)) if SPANS[s][0] <= j0)
             c0 = j0 - SPANS[s][0]
-            z = keep.tile([P, n, PACK], BF16, name="z%d" % i, align_bytes=64)
+            z = keep.tile([P, n, PACK], BF16, name="z%d" % i, align_bytes=256)
             nc.scalar.activation(
                 z[:].rearrange("p (c i) t -> p c t i", i=4),
                 conv[s][:, :, c0 : c0 + n].rearrange("p t (c i) -> p c t i", i=4),
@@ -185,17 +183,15 @@ def tile_picked_dconv_silu_p_kernel(
 
         def project(i):
             j0, n = PIECES[i]
-            codes = keep.tile([P, n], U32, name="z_codes%d" % i, align_bytes=64)
-            plane = keep.tile([P, n], U8, name="z_plane%d" % i, align_bytes=64)
+            codes = keep.tile([P, n], U32, name="z_codes%d" % i, align_bytes=256)
+            plane = keep.tile([P, n], U8, name="z_plane%d" % i, align_bytes=256)
             nc.vector.quantize_mx(
                 out=codes[:].bitcast(FP8X4), scales=plane[:], in_=z_tiles[i][:].rearrange("p n t -> p (n t)")
             )
             if WAY_OUT[i] == "both":
                 accs = [psum.tile([P, HALF], F32, name="y%d_%d" % (i, m), tag="bank")[:, 0:n] for m in range(2)]
             else:
-                y = early.get(i)
-                if y is None:
-                    y = psum.tile([P, HALF], F32, name="y%d" % i, tag="bank")
+                y = psum.tile([P, HALF], F32, name="y%d" % i, tag="bank")
                 accs = [y[:, m * n : (m + 1) * n] for m in range(2)] + [y[:, 0 : 2 * n]]
             for m in range(2):
                 nc.tensor.matmul_mx(
@@ -208,23 +204,10 @@ def tile_picked_dconv_silu_p_kernel(
                     stop=True,
                 )
             products[i] = accs
-            if i == REWARM_AFTER:
-                spare = psum.tile([P, HALF], F32, name="y%d" % (i + 1), tag="bank")
-                early[i + 1] = spare
-                for warm in range(REWARM_PASSES):
-                    nc.tensor.matmul_mx(
-                        out=spare[0:WARM_ROWS, 2 * n : 3 * n],
-                        lhsT=w2_codes[:, 0:WARM_ROWS].bitcast(FP8X4),
-                        lhsT_scale=w2_plane[:, 0:WARM_ROWS],
-                        rhs=codes[:].bitcast(FP8X4),
-                        rhs_scale=plane[:],
-                        start=True,
-                        stop=True,
-                    )
 
         def store(i):
             j0, n = PIECES[i]
-            staged = keep.tile([P, 2 * n], F32, name="staged%d" % i, align_bytes=64)
+            staged = keep.tile([P, 2 * n], F32, name="staged%d" % i, align_bytes=256)
             accs = products[i]
             if WAY_OUT[i] == "both":
                 nc.scalar.copy(staged[:, 0:n], accs[0])

@@ -138,7 +138,7 @@ def tile_picked_dconv_silu_p_kernel(
                 stop=True,
             )
 
-        conv = [keep.tile([P, PACK, n], F32, name="conv%d" % j0, align_bytes=256) for j0, n in SPANS]
+        conv = [keep.tile([P, n // 4, PACK, 4], F32, name="conv%d" % j0, align_bytes=256) for j0, n in SPANS]
 
         def lag(b):
             half, t = divmod(b, PACK)
@@ -152,10 +152,10 @@ def tile_picked_dconv_silu_p_kernel(
             j0, n = SPANS[s]
             for t in range(PACK):
                 nc.vector.scalar_tensor_tensor(
-                    conv[s][:, t, :],
-                    banks[PACK * (j0 // HALF) + t][:, j0 % HALF : j0 % HALF + n],
+                    conv[s][:, :, t, :],
+                    banks[PACK * (j0 // HALF) + t][:, j0 % HALF : j0 % HALF + n].rearrange("p (c i) -> p c i", i=4),
                     tap_cols[:, t, 0:1],
-                    lagged[:, t, PAD - 1 + j0 : PAD - 1 + j0 + n],
+                    lagged[:, t, PAD - 1 + j0 : PAD - 1 + j0 + n].rearrange("p (c i) -> p c i", i=4),
                     MULT,
                     ADD,
                 )
@@ -176,7 +176,7 @@ def tile_picked_dconv_silu_p_kernel(
             z = keep.tile([P, n, PACK], BF16, name="z%d" % i, align_bytes=256)
             nc.scalar.activation(
                 z[:].rearrange("p (c i) t -> p c t i", i=4),
-                conv[s][:, :, c0 : c0 + n].rearrange("p t (c i) -> p c t i", i=4),
+                conv[s][:, c0 // 4 : (c0 + n) // 4, :, :],
                 SILU,
             )
             z_tiles[i] = z

@@ -57,7 +57,7 @@ def tile_picked_dconv_silu_p_kernel(
         )
 
         tap_cols = keep.tile([P, PACK, 2], F32, name="tap_cols")
-        nc.scalar.dma_start(tap_cols[:], taps.rearrange("(p t) d -> p t d", t=PACK))
+        nc.sync.dma_start(tap_cols[:], taps.rearrange("(p t) d -> p t d", t=PACK))
 
         x_plane = keep.tile([P, S], U8, name="x_plane", align_bytes=256)
         nc.vector.memset(x_plane[:].bitcast(I32), 0)
@@ -169,25 +169,27 @@ def tile_picked_dconv_silu_p_kernel(
 
         z_tiles, products = {}, {}
 
-        def silu(i):
-            j0, n = PIECES[i]
+        def silu_and_quantise(first, count):
+            j0, n = first * 128, count * 128
             s = max(s for s in range(len(SPANS)) if SPANS[s][0] <= j0)
             c0 = j0 - SPANS[s][0]
-            z = keep.tile([P, n, PACK], BF16, name="z%d" % i, align_bytes=256)
+            z = keep.tile([P, n, PACK], BF16, name="z%d" % first, align_bytes=256)
             nc.scalar.activation(
                 z[:].rearrange("p (c i) t -> p c t i", i=4),
                 conv[s][:, c0 // 4 : (c0 + n) // 4, :, :],
                 SILU,
             )
-            z_tiles[i] = z
+            codes = keep.tile([P, n], U32, name="z_codes%d" % first, align_bytes=256)
+            plane = keep.tile([P, n], U8, name="z_plane%d" % first, align_bytes=256)
+            nc.vector.quantize_mx(
+                out=codes[:].bitcast(FP8X4), scales=plane[:], in_=z[:].rearrange("p n t -> p (n t)")
+            )
+            for k in range(count):
+                z_tiles[first + k] = (codes[:, k * 128 : (k + 1) * 128], plane[:, k * 128 : (k + 1) * 128])
 
         def project(i):
             j0, n = PIECES[i]
-            codes = keep.tile([P, n], U32, name="z_codes%d" % i, align_bytes=256)
-            plane = keep.tile([P, n], U8, name="z_plane%d" % i, align_bytes=256)
-            nc.vector.quantize_mx(
-                out=codes[:].bitcast(FP8X4), scales=plane[:], in_=z_tiles[i][:].rearrange("p n t -> p (n t)")
-            )
+            codes, plane = z_tiles[i]
             if WAY_OUT[i] == "both":
                 accs = [psum.tile([P, HALF], F32, name="y%d_%d" % (i, m), tag="bank")[:, 0:n] for m in range(2)]
             else:
@@ -198,8 +200,8 @@ def tile_picked_dconv_silu_p_kernel(
                     out=accs[m],
                     lhsT=w2_codes[:, m * P : (m + 1) * P].bitcast(FP8X4),
                     lhsT_scale=w2_plane[:, m * P : (m + 1) * P],
-                    rhs=codes[:].bitcast(FP8X4),
-                    rhs_scale=plane[:],
+                    rhs=codes.bitcast(FP8X4),
+                    rhs_scale=plane,
                     start=True,
                     stop=True,
                 )
@@ -210,9 +212,9 @@ def tile_picked_dconv_silu_p_kernel(
             staged = keep.tile([P, 2 * n], F32, name="staged%d" % i, align_bytes=256)
             accs = products[i]
             if WAY_OUT[i] == "both":
-                nc.scalar.copy(staged[:, 0:n], accs[0])
+                nc.vector.tensor_copy(staged[:, 0:n], accs[0])
                 nc.sync.dma_start(out[0:P, j0 : j0 + n], staged[:, 0:n])
-                nc.vector.tensor_copy(staged[:, n : 2 * n], accs[1])
+                nc.scalar.copy(staged[:, n : 2 * n], accs[1])
                 nc.sync.dma_start(out[P : 2 * P, j0 : j0 + n], staged[:, n : 2 * n])
                 return
             elif WAY_OUT[i] == "scalar":
@@ -224,10 +226,11 @@ def tile_picked_dconv_silu_p_kernel(
                 staged[:].rearrange("p (m n) -> p m n", m=2),
             )
 
-        for i in range(len(PIECES)):
-            if i == 2:
+        for first, count in ((0, 2), (2, 2), (4, 1), (5, 1), (6, 1), (7, 1)):
+            if first == 2:
                 combine(2)
-            silu(i)
-            project(i)
+            silu_and_quantise(first, count)
+            for i in range(first, first + count):
+                project(i)
         for i in range(len(PIECES)):
             store(i)

from contextlib import ExitStack

import concourse.mybir as mybir

K, T, S, H, N = 512, 4096, 1024, 512, 256
FLOPS = 2 * K * H * S + 2 * H * N * S

F32 = mybir.dt.float32
BF16 = mybir.dt.bfloat16
I32 = mybir.dt.int32
U32 = mybir.dt.uint32
U16 = mybir.dt.uint16
U8 = mybir.dt.uint8
FP8X4 = mybir.dt.float8_e4m3fn_x4
MULT = mybir.AluOpType.mult
ADD = mybir.AluOpType.add
COPY = mybir.ActivationFunctionType.Copy
SILU = mybir.ActivationFunctionType.Silu

P = 128
PACK = 4
HALF = 512
PAD = 4
WARM_PASSES = 3
WARM_ROWS = 32
ROW0, ROW_STEP = 11, 7
VECTOR_BANKS = (1, 7)
SPANS = ((0, 512), (512, 256), (768, 256))
PIECES = tuple((128 * i, 128) for i in range(8))
WAY_OUT = ("vector",) * 4 + ("scalar",) * 3 + ("both",)


def tile_picked_dconv_silu_p_kernel(
    tc, x_words, x_scales, w1, w2_words, w2_scales, taps, offs, out
):
    nc = tc.nc
    with ExitStack() as ctx:
        keep = ctx.enter_context(tc.tile_pool(name="keep", bufs=1))
        psum = ctx.enter_context(tc.psum_pool(name="psum", bufs=8))

        w1_rows = w1.rearrange("(p j) c -> p j c", j=PACK)
        w1_raw = keep.tile([P, PACK, H], F32, name="w1_raw", tag="w1_raw", align_bytes=256)
        nc.sync.dma_start(w1_raw[:, 0:2, :], w1_rows[:, 0:2, :])

        offsets = keep.tile([P, S // 16], U16, name="offsets")
        nc.sync.dma_start(offsets[:], offs)

        scale_table = keep.tile([P, T], U8, name="scale_table", tag="scale_table", align_bytes=256)
        nc.vector.memset(scale_table[:].bitcast(I32), 0)
        nc.sync.dma_start(scale_table[:].bitcast(I32)[ROW0 : ROW0 + 16 * ROW_STEP : ROW_STEP, :], x_scales[0].bitcast(I32))

        nc.sync.dma_start(w1_raw[:, 2:4, :], w1_rows[:, 2:4, :])

        word_table = keep.tile([P, T], U32, name="word_table", align_bytes=256)
        nc.sync.dma_start(
            word_table[:].bitcast(I32), x_words[0].rearrange("p c r -> p (c r)").bitcast(I32)
        )

        tap_cols = keep.tile([P, PACK, 2], F32, name="tap_cols")
        nc.sync.dma_start(tap_cols[:], taps.rearrange("(p t) d -> p t d", t=PACK))

        x_plane = keep.tile([P, S], U8, name="x_plane", align_bytes=256)
        nc.vector.memset(x_plane[:].bitcast(I32), 0)

        lagged = keep.tile([P, PACK, PAD + S], F32, name="lagged", align_bytes=256)
        zeros = keep.tile([P, PACK, PAD], F32, name="zeros")
        nc.vector.memset(zeros[:], 0.0)
        nc.scalar.activation(lagged[:, :, 0:PAD], zeros[:], SILU)

        picked_scales = keep.tile([P, S], U8, name="picked_scales", align_bytes=256)
        nc.vector.tensor_copy(picked_scales[:], scale_table[:].indirect(offsets[:]))
        for q in range(4):
            nc.sync.dma_start(
                x_plane[:].bitcast(I32)[32 * q : 32 * q + 4, :],
                picked_scales[:].bitcast(I32)[ROW0 + 4 * q * ROW_STEP : ROW0 + 4 * (q + 1) * ROW_STEP : ROW_STEP, :],
            )

        w2_plane = keep.tile([P, N], U8, name="w2_plane", tag="scale_table", align_bytes=256)
        nc.vector.memset(w2_plane[:].bitcast(I32), 0)
        for q in range(4):
            nc.sync.dma_start(
                w2_plane[:].bitcast(I32)[32 * q : 32 * q + 4, :], w2_scales[0].bitcast(I32)[4 * q : 4 * q + 4, :]
            )

        w1_src = w1_raw[:].rearrange("p j (m t) -> p m j t", t=PACK)
        first_groups = keep.tile([P, PACK - 1, P, PACK], BF16, name="first_groups", align_bytes=256)
        last_group = keep.tile([P, P, PACK], BF16, name="last_group", align_bytes=256)
        nc.scalar.copy(first_groups[:].rearrange("p t m j -> p m j t"), w1_src[:, :, :, 0 : PACK - 1])
        nc.vector.tensor_copy(last_group[:], w1_src[:, :, :, PACK - 1])

        w2_codes = keep.tile([P, N], U32, name="w2_codes", tag="w1_raw", align_bytes=256)
        nc.sync.dma_start(
            w2_codes[:].bitcast(I32), w2_words[0].rearrange("p c r -> p (c r)").bitcast(I32)
        )

        w1_codes = keep.tile([P, PACK, P], U32, name="w1_codes", align_bytes=256)
        w1_plane = keep.tile([P, PACK, P], U8, name="w1_plane", align_bytes=256)
        nc.vector.quantize_mx(
            out=w1_codes[:, PACK - 1, :].bitcast(FP8X4),
            scales=w1_plane[:, PACK - 1, :],
            in_=last_group[:].rearrange("p m j -> p (m j)"),
        )
        for t0, t1 in ((0, 2), (2, 3)):
            nc.vector.quantize_mx(
                out=w1_codes[:, t0:t1, :].rearrange("p t m -> p (t m)").bitcast(FP8X4),
                scales=w1_plane[:, t0:t1, :].rearrange("p t m -> p (t m)"),
                in_=first_groups[:, t0:t1, :, :].rearrange("p t m j -> p (t m j)"),
            )

        banks = [psum.tile([P, HALF], F32, name="h%d" % b, tag="bank") for b in range(8)]
        for warm in range(WARM_PASSES):
            nc.tensor.matmul_mx(
                out=banks[7][0:WARM_ROWS, :],
                lhsT=w1_codes[:, 0, 0:WARM_ROWS].bitcast(FP8X4),
                lhsT_scale=w1_plane[:, 0, 0:WARM_ROWS],
                rhs=w1_codes[:].rearrange("p t m -> p (t m)").bitcast(FP8X4),
                rhs_scale=w1_plane[:].rearrange("p t m -> p (t m)"),
                start=True,
                stop=True,
            )

        picked = []
        for half in range(2):
            words = keep.tile([P, HALF], U32, name="picked%d" % half, align_bytes=256)
            cols = slice(half * HALF // 16, (half + 1) * HALF // 16)
            nc.vector.tensor_copy(words[:], word_table[:].indirect(offsets[:, cols]))
            picked.append(words)

        for b in range(8):
            half, t = divmod(b, PACK)
            nc.tensor.matmul_mx(
                out=banks[b][:],
                lhsT=w1_codes[:, t, :].bitcast(FP8X4),
                lhsT_scale=w1_plane[:, t, :],
                rhs=picked[half][:].bitcast(FP8X4),
                rhs_scale=x_plane[:, half * HALF : (half + 1) * HALF],
                start=True,
                stop=True,
            )

        conv = [keep.tile([P, n // 4, PACK, 4], F32, name="conv%d" % j0, align_bytes=256) for j0, n in SPANS]

        def lag(b):
            half, t = divmod(b, PACK)
            dst = lagged[:, t, PAD + half * HALF : PAD + (half + 1) * HALF]
            if b in VECTOR_BANKS:
                nc.vector.tensor_scalar(dst, banks[b][:], tap_cols[:, t, 1:2], None, MULT)
            else:
                nc.scalar.activation(dst, banks[b][:], COPY, scale=tap_cols[:, t, 1:2])

        def combine(s):
            j0, n = SPANS[s]
            for t in range(PACK):
                nc.vector.scalar_tensor_tensor(
                    conv[s][:, :, t, :],
                    banks[PACK * (j0 // HALF) + t][:, j0 % HALF : j0 % HALF + n].rearrange("p (c i) -> p c i", i=4),
                    tap_cols[:, t, 0:1],
                    lagged[:, t, PAD - 1 + j0 : PAD - 1 + j0 + n].rearrange("p (c i) -> p c i", i=4),
                    MULT,
                    ADD,
                )

        for b in range(PACK):
            lag(b)
        combine(0)
        for b in range(PACK, 2 * PACK):
            lag(b)
        combine(1)

        z_tiles, products = {}, {}

        def silu_and_quantise(first, count):
            j0, n = first * 128, count * 128
            s = max(s for s in range(len(SPANS)) if SPANS[s][0] <= j0)
            c0 = j0 - SPANS[s][0]
            z = keep.tile([P, n, PACK], BF16, name="z%d" % first, align_bytes=256)
            nc.scalar.activation(
                z[:].rearrange("p (c i) t -> p c t i", i=4),
                conv[s][:, c0 // 4 : (c0 + n) // 4, :, :],
                SILU,
            )
            codes = keep.tile([P, n], U32, name="z_codes%d" % first, align_bytes=256)
            plane = keep.tile([P, n], U8, name="z_plane%d" % first, align_bytes=256)
            nc.vector.quantize_mx(
                out=codes[:].bitcast(FP8X4), scales=plane[:], in_=z[:].rearrange("p n t -> p (n t)")
            )
            for k in range(count):
                z_tiles[first + k] = (codes[:, k * 128 : (k + 1) * 128], plane[:, k * 128 : (k + 1) * 128])

        def project(i):
            j0, n = PIECES[i]
            codes, plane = z_tiles[i]
            if WAY_OUT[i] == "both":
                accs = [psum.tile([P, HALF], F32, name="y%d_%d" % (i, m), tag="bank")[:, 0:n] for m in range(2)]
            else:
                y = psum.tile([P, HALF], F32, name="y%d" % i, tag="bank")
                accs = [y[:, m * n : (m + 1) * n] for m in range(2)] + [y[:, 0 : 2 * n]]
            for m in range(2):
                nc.tensor.matmul_mx(
                    out=accs[m],
                    lhsT=w2_codes[:, m * P : (m + 1) * P].bitcast(FP8X4),
                    lhsT_scale=w2_plane[:, m * P : (m + 1) * P],
                    rhs=codes.bitcast(FP8X4),
                    rhs_scale=plane,
                    start=True,
                    stop=True,
                )
            products[i] = accs

        def store(i):
            j0, n = PIECES[i]
            staged = keep.tile([P, 2 * n], F32, name="staged%d" % i, align_bytes=256)
            accs = products[i]
            if WAY_OUT[i] == "both":
                nc.vector.tensor_copy(staged[:, 0:n], accs[0])
                nc.sync.dma_start(out[0:P, j0 : j0 + n], staged[:, 0:n])
                nc.scalar.copy(staged[:, n : 2 * n], accs[1])
                nc.sync.dma_start(out[P : 2 * P, j0 : j0 + n], staged[:, n : 2 * n])
                return
            elif WAY_OUT[i] == "scalar":
                nc.scalar.copy(staged[:], accs[2])
            else:
                nc.vector.tensor_copy(staged[:], accs[2])
            nc.sync.dma_start(
                out[:, j0 : j0 + n].rearrange("(m p) n -> p m n", p=P),
                staged[:].rearrange("p (m n) -> p m n", m=2),
            )

        for first, count in ((0, 2), (2, 2), (4, 1), (5, 1), (6, 1), (7, 1)):
            if first == 2:
                combine(2)
            silu_and_quantise(first, count)
            for i in range(first, first + count):
                project(i)
        for i in range(len(PIECES)):
            store(i)
